import numpy as np
import ml_dtypes


def mxq(x, axis, fmt="e4m3"):
    dtype, down = {"e4m3": (ml_dtypes.float8_e4m3fn, 7), "e5m2": (ml_dtypes.float8_e5m2, 14)}[fmt]
    v = np.moveaxis(np.asarray(x, np.float32).astype(ml_dtypes.bfloat16).astype(np.float64), axis, -1)
    blocks = v.reshape(v.shape[:-1] + (-1, 32))
    amax = np.abs(blocks).max(-1, keepdims=True)
    byte = np.maximum(np.where(amax > 0, np.frexp(amax)[1] - 1 + 127, 0) - down, 1)
    scale = np.exp2(byte - 127.0)
    codes = (blocks / scale).astype(np.float32).astype(dtype).astype(np.float64)
    return np.moveaxis((codes * scale).reshape(v.shape), -1, axis)


WIDE = False


def mx_kscale(k):
    if not WIDE:
        return np.ones(k)
    levels = np.array([10, -10, 5, -5, 0])
    if k % 512:
        return np.exp2(np.random.permutation(np.resize(levels, k // 32))).repeat(32)
    a = np.empty((k // 512, 16))
    for p in range(k // 512):
        a[p, :8] = np.random.permutation(np.resize(levels, 8))
        for g in range(8):
            far = levels[np.abs(levels - a[p, g]) >= 10]
            a[p, g + 8] = far[np.random.randint(len(far))]
    return np.exp2(a.ravel()).repeat(32)


def f64(x):
    return np.asarray(x).astype(np.float64)


def striped(idx):
    return np.tile(idx.reshape(-1, 16).T, (8, 1)).astype(np.uint16)


def unstriped(offs):
    return offs[:16].T.reshape(-1).astype(np.int64)


E2M1 = np.array([0.0, 0.5, 1.0, 1.5, 2.0, 3.0, 4.0, 6.0, -0.0, -0.5, -1.0, -1.5, -2.0, -3.0, -4.0, -6.0])


def pack_weight(w, fmt):
    k, n = w.shape
    w = f64(np.asarray(w, np.float32).astype(ml_dtypes.bfloat16)).reshape(k // 32, 32, n)
    amax = np.abs(w).max(1)
    if fmt == "e4m3":
        byte = np.frexp(amax)[1] - 1 + 127 - 7
    else:
        mant, ex = np.frexp(amax / 6.0)
        byte = np.where(mant > 0.5, ex, ex - 1) + 127
    byte = np.clip(np.where(amax > 0, byte, 1), 1, 254)
    scaled = (w * np.exp2(127.0 - byte)[:, None, :]).reshape(k, n).astype(np.float32)
    by_word = np.ascontiguousarray(scaled.reshape(k // 512, 128, 4, n).transpose(0, 1, 3, 2))
    if fmt == "e4m3":
        words = by_word.astype(ml_dtypes.float8_e4m3fn).view(np.uint8)
    else:
        c = by_word.astype(ml_dtypes.float4_e2m1fn).view(np.uint8) & 0xF
        words = (c[..., 0::2] | (c[..., 1::2] << 4)).reshape(k // 512, 128, 2 * n)
    return np.ascontiguousarray(words), np.ascontiguousarray(byte.astype(np.uint8).reshape(k // 512, 16, n))


def unpack_weight(words, scales, fmt):
    g, _, n = scales.shape
    words = np.ascontiguousarray(words).reshape(g, 128, n, -1)
    if fmt == "e4m3":
        vals = words.view(ml_dtypes.float8_e4m3fn).astype(np.float64)
    else:
        nib = np.empty((g, 128, n, 4), np.uint8)
        nib[..., 0::2] = words & 0xF
        nib[..., 1::2] = words >> 4
        vals = E2M1[nib]
    vals = vals * np.repeat(np.exp2(scales.astype(np.float64) - 127.0), 8, axis=1)[..., None]
    return vals.transpose(0, 1, 3, 2).reshape(g * 512, n)


def d_silu(v):
    s = 1.0 / (1.0 + np.exp(-np.maximum(v, -700.0)))
    return s * (1.0 + v * (1.0 - s))


K, T, E, C, H, N = 256, 512, 8, 128, 512, 512


def by_expert(wq, xq):
    return np.concatenate([wq[e].T @ xq[:, e * C:(e + 1) * C] for e in range(E)], axis=1)


def setup_inputs():
    n = np.random.standard_normal
    s = mx_kscale(N)[:, None]
    u = mx_kscale(H)
    first = np.random.permutation(np.repeat(np.arange(E), T // E))
    second = (first + 1 + np.random.permutation(np.repeat(np.arange(E - 1), -(-T // (E - 1)))[:T])) % E
    while np.bincount(second, minlength=E).max() != T // E:
        load = np.bincount(second, minlength=E); hi, lo = int(load.argmax()), int(load.argmin())
        t = np.flatnonzero((second == hi) & (first != lo))[0]; second[t] = lo
    slot_token = np.empty(E * C, np.int64); pos = np.empty((2, T), np.int64); fill = np.zeros(E, np.int64)
    place = np.stack([np.random.permutation(C) for _ in range(E)])
    for r, deal in enumerate((first, second)):
        for t in np.random.permutation(T):
            e = deal[t]; j = e * C + place[e, fill[e]]; fill[e] += 1; slot_token[j] = t; pos[r, t] = j
    g = np.random.uniform(0.2, 0.8, T)
    w_slot = np.empty(E * C); w_slot[pos[0]] = g; w_slot[pos[1]] = 1.0 - g
    w2 = [pack_weight(m, "e2m1") for m in n((E, N, H)) / np.sqrt(N) / s[None] * u[None, None, :]]
    w1 = [pack_weight(m, "e2m1") for m in n((E, H, K)) / np.sqrt(H) / u[None, :, None]]
    return {
        "dyT": (n((N, T)) * s).astype(np.float32),
        "a": n((H, E * C)).astype(np.float32),
        "w2_words": np.stack([m[0] for m in w2]),
        "w2_scales": np.stack([m[1] for m in w2]),
        "w1_words": np.stack([m[0] for m in w1]),
        "w1_scales": np.stack([m[1] for m in w1]),
        "gate": np.tile(w_slot, (N, 1)).astype(np.float32),
        "offs": striped(slot_token),
        "pos1": striped(pos[0]),
        "pos2": striped(pos[1]),
    }


def reference(dyT, a, w2_words, w2_scales, w1_words, w1_scales, gate, offs, pos1, pos2):
    idx = unstriped(offs)
    w2 = np.stack([unpack_weight(w2_words[e], w2_scales[e], "e2m1") for e in range(E)])
    w1 = np.stack([unpack_weight(w1_words[e], w1_scales[e], "e2m1") for e in range(E)])
    gq = mxq(f64(gate) * f64(dyT)[:, idx], 0, "e4m3")
    dh = by_expert(w2, gq)
    da = dh * d_silu(f64(a))
    dx = by_expert(w1, mxq(da, 0, "e4m3"))
    return dx[:, unstriped(pos1)] + dx[:, unstriped(pos2)]

@@ -1,0 +1,285 @@
+from contextlib import ExitStack
+
+import concourse.mybir as mybir
+from concourse.masks import make_identity
+
+K, T, E, C, H, N = 256, 512, 8, 128, 512, 512
+S = E * C
+FLOPS = 2 * S * (N * H + H * K)
+BYTES = 4 * (N * T + H * S + S + K * T) + E * (2 * 128 * H + 16 * H + 2 * 128 * K + 16 * K) + 2 * 128 * (S // 16 + 2 * (T // 16))
+
+F32 = mybir.dt.float32
+BF16 = mybir.dt.bfloat16
+I32 = mybir.dt.int32
+U32 = mybir.dt.uint32
+U16 = mybir.dt.uint16
+U8 = mybir.dt.uint8
+FP8X4 = mybir.dt.float8_e4m3fn_x4
+FP4X4 = mybir.dt.float4_e2m1fn_x4
+
+ADD, MULT, SUB = mybir.AluOpType.add, mybir.AluOpType.mult, mybir.AluOpType.subtract
+SIGMOID, SILU = mybir.ActivationFunctionType.Sigmoid, mybir.ActivationFunctionType.Silu
+
+P = 128
+PACK = 4
+CHUNK = 256
+CHUNKS = S // CHUNK
+PER_CHUNK = CHUNK // C
+
+
+def tile_moe_bdx_mlp_silu_kernel(tc, dyT, a, w2_words, w2_scales, w1_words, w1_scales, gate, offs, pos1, pos2, out):
+    nc = tc.nc
+    with ExitStack() as ctx:
+        lists = ctx.enter_context(tc.tile_pool(name="lists", bufs=1))
+        keep = ctx.enter_context(tc.tile_pool(name="keep", bufs=1))
+        work = ctx.enter_context(tc.tile_pool(name="work", bufs=3))
+        psum = ctx.enter_context(tc.psum_pool(name="psum", bufs=1))
+
+        offs_sb = lists.tile([P, S // 16], U16, name="offs_sb")
+        pos1_sb = lists.tile([P, T // 16], U16, name="pos1_sb")
+        pos2_sb = lists.tile([P, T // 16], U16, name="pos2_sb")
+
+        warm = keep.tile([P, 8], F32, name="warm")
+        nc.vector.memset(warm[:], 0.0)
+        warmed = keep.tile([P, 8], F32, name="warmed")
+        nc.scalar.activation(warmed[:], warm[:], SIGMOID)
+
+        w2_sb = keep.tile([P, E, 2 * H], U8, name="w2_sb", align_bytes=64)
+        w2s_sb = keep.tile([P, E, H], U8, name="w2s_sb", align_bytes=64)
+        w1_sb = keep.tile([P, E, 2 * K], U8, name="w1_sb", align_bytes=64)
+        w1s_sb = keep.tile([P, E, K], U8, name="w1s_sb", align_bytes=64)
+        nc.vector.memset(w2s_sb[:].rearrange("p e i -> p (e i)").bitcast(I32), 0)
+        nc.vector.memset(w1s_sb[:].rearrange("p e k -> p (e k)").bitcast(I32), 0)
+        ident = keep.tile([P, P], F32, name="ident")
+        make_identity(nc, ident[:])
+
+        gate_sb = keep.tile([P, S], F32, name="gate_sb")
+        dy = []
+        for t in range(PACK):
+            dy_t = keep.tile([P, T], F32, name=f"dy{t}")
+            dy.append(dy_t)
+        a_sb, r_sb, s_sb, d_sb = [], [], [], []
+        for c in range(CHUNKS):
+            a_c = keep.tile([P, PACK, CHUNK], F32, name=f"a{c}")
+            r_c = keep.tile([P, PACK, CHUNK], F32, name=f"r{c}")
+            s_c = keep.tile([P, PACK, CHUNK], F32, name=f"s{c}")
+            d_c = keep.tile([P, PACK, CHUNK], F32, name=f"d{c}")
+            a_sb.append(a_c)
+            r_sb.append(r_c)
+            s_sb.append(s_c)
+            d_sb.append(d_c)
+
+        dy_hbm = dyT.rearrange("(p t) s -> p t s", t=PACK)
+        a_hbm = a.rearrange("(p t) s -> p t s", t=PACK)
+
+        def load_gate(lo, hi):
+            nc.sync.dma_start(out=gate_sb[:, lo:hi], in_=gate[0:P, lo:hi])
+
+        def load_dy(t):
+            nc.sync.dma_start(out=dy[t][:], in_=dy_hbm[:, t, :])
+
+        def load_a(c):
+            nc.sync.dma_start(out=a_sb[c][:], in_=a_hbm[:, :, c * CHUNK : (c + 1) * CHUNK])
+
+        def load_words(tile, words, lo, hi):
+            nc.sync.dma_start(out=tile[:, lo:hi, :].bitcast(I32), in_=words.rearrange("e s p c -> p (e s) c")[:, lo:hi, :].bitcast(I32))
+
+        def load_scales(tile, scales):
+            rows = scales.rearrange("e s f i -> f (e s) i")
+            for q in range(4):
+                nc.sync.dma_start(out=tile[q:P:32, :, :].bitcast(I32), in_=rows[q:16:4, :, :].bitcast(I32))
+
+        nc.sync.dma_start(offs_sb[:], offs)
+        load_dy(0)
+        load_dy(1)
+        load_dy(2)
+        load_dy(3)
+        load_a(0)
+        load_gate(0, 2 * CHUNK)
+        load_scales(w2s_sb, w2_scales)
+        load_words(w2_sb, w2_words, 0, 2)
+        load_a(1)
+        load_gate(2 * CHUNK, S)
+        load_a(2)
+        load_words(w2_sb, w2_words, 2, 4)
+        load_a(3)
+        load_words(w2_sb, w2_words, 4, 8)
+        load_scales(w1s_sb, w1_scales)
+        load_words(w1_sb, w1_words, 0, 8)
+        nc.sync.dma_start(pos1_sb[:], pos1)
+        nc.sync.dma_start(pos2_sb[:], pos2)
+
+        dhT_ps, dhT_sb, dh_ps, dab, daq, das, dx_ps = {}, {}, {}, {}, {}, {}, {}
+        g4, gb, gq, gs = {}, {}, {}, {}
+        dx_sb = keep.tile([P, 2, S], F32, name="dx_sb")
+
+        def cols(c):
+            return slice(c * CHUNK, (c + 1) * CHUNK)
+
+        def idx(c):
+            return offs_sb[:, c * CHUNK // 16 : (c + 1) * CHUNK // 16]
+
+        def new_g4(c):
+            tile = work.tile([P, PACK, CHUNK], F32, name="g4")
+            g4[c] = tile
+
+        def gather_copy(c, t):
+            nc.vector.tensor_copy(g4[c][:, t, :], dy[t][:].indirect(idx(c)))
+
+        def gather_mul(c, t):
+            nc.vector.tensor_tensor(out=g4[c][:, t, :], in0=dy[t][:].indirect(idx(c)), in1=gate_sb[:, cols(c)], op=MULT)
+
+        def new_gb(c):
+            tile = work.tile([P, CHUNK, PACK], BF16, name="gb", align_bytes=64)
+            gb[c] = tile
+
+        def interleave(c):
+            new_gb(c)
+            nc.scalar.copy(gb[c][:], g4[c][:].rearrange("p t s -> p s t"))
+
+        def gate_interleave(c, parts):
+            new_gb(c)
+            n = CHUNK // parts
+            for k in range(parts):
+                lo = k * n
+                nc.gpsimd.tensor_tensor(
+                    out=gb[c][:, lo : lo + n, :],
+                    in0=g4[c][:, :, lo : lo + n].rearrange("p t s -> p s t"),
+                    in1=gate_sb[:, c * CHUNK + lo : c * CHUNK + lo + n].unsqueeze(2).to_broadcast([P, n, PACK]),
+                    op=MULT,
+                )
+
+        def quantize_g(c):
+            words = work.tile([P, CHUNK], U32, name="gq", align_bytes=64)
+            scales = work.tile([P, CHUNK], U8, name="gs", align_bytes=64)
+            nc.vector.quantize_mx(out=words[:].bitcast(FP8X4), scales=scales[:], in_=gb[c][:].rearrange("p s t -> p (s t)"))
+            gq[c], gs[c] = words, scales
+
+        def sigmoid(c):
+            nc.scalar.activation(r_sb[c][:], a_sb[c][:], SIGMOID)
+
+        def silu(c):
+            nc.scalar.activation(s_sb[c][:], a_sb[c][:], SILU, scale=-1.0)
+
+        def silu_on_vector(c):
+            nc.vector.scalar_tensor_tensor(out=s_sb[c][:], in0=r_sb[c][:], scalar=1.0, in1=a_sb[c][:], op0=SUB, op1=MULT)
+
+        def slope(c):
+            nc.vector.scalar_tensor_tensor(out=d_sb[c][:], in0=s_sb[c][:], scalar=1.0, in1=r_sb[c][:], op0=SUB, op1=MULT)
+
+        def mm1(e):
+            c, j = divmod(e, PER_CHUNK)
+            tile = psum.tile([P, H], F32, name="dhT_ps", bufs=3)
+            nc.tensor.matmul_mx(
+                out=tile[:],
+                lhsT=gq[c][:, j * C : (j + 1) * C].bitcast(FP8X4),
+                lhsT_scale=gs[c][:, j * C : (j + 1) * C],
+                rhs=w2_sb[:, e, :].bitcast(FP4X4),
+                rhs_scale=w2s_sb[:, e, :],
+                start=True,
+                stop=True,
+            )
+            dhT_ps[e] = tile
+
+        def evac(e):
+            tile = work.tile([P, PACK, P], F32, name="dhT", bufs=4)
+            nc.scalar.copy(tile[:], dhT_ps[e][:].rearrange("s (m t) -> s t m", t=PACK))
+            dhT_sb[e] = tile
+
+        def turn(e):
+            tile = psum.tile([P, PACK, C], F32, name="dh_ps", bufs=3)
+            for t in range(PACK):
+                nc.tensor.transpose(tile[:, t, :], dhT_sb[e][:, t, :], ident[:])
+            dh_ps[e] = tile
+
+        def times_slope(e):
+            c, j = divmod(e, PER_CHUNK)
+            tile = work.tile([P, C, PACK], BF16, name="dab", align_bytes=64)
+            nc.vector.scalar_tensor_tensor(
+                out=tile[:],
+                in0=dh_ps[e][:].rearrange("p t s -> p s t"),
+                scalar=-1.0,
+                in1=d_sb[c][:, :, j * C : (j + 1) * C].rearrange("p t s -> p s t"),
+                op0=MULT,
+                op1=MULT,
+            )
+            dab[e] = tile
+
+        def quantize_da(e):
+            words = work.tile([P, C], U32, name="daq", align_bytes=64)
+            scales = work.tile([P, C], U8, name="das", align_bytes=64)
+            nc.vector.quantize_mx(out=words[:].bitcast(FP8X4), scales=scales[:], in_=dab[e][:].rearrange("p s t -> p (s t)"))
+            daq[e], das[e] = words, scales
+
+        def mm2(e):
+            c, j = divmod(e, PER_CHUNK)
+            if j == 0:
+                tile = psum.tile([P, 2, CHUNK], F32, name="dx_ps", bufs=2)
+                dx_ps[c] = tile
+            for kt in range(2):
+                nc.tensor.matmul_mx(
+                    out=dx_ps[c][:, kt, j * C : (j + 1) * C],
+                    lhsT=w1_sb[:, e, kt * 2 * P : (kt + 1) * 2 * P].bitcast(FP4X4),
+                    lhsT_scale=w1s_sb[:, e, kt * P : (kt + 1) * P],
+                    rhs=daq[e][:].bitcast(FP8X4),
+                    rhs_scale=das[e][:],
+                    start=True,
+                    stop=True,
+                )
+
+        def store_slots(c):
+            nc.scalar.copy(dx_sb[:, :, cols(c)], dx_ps[c][:])
+
+        def store_slots_part(c, j):
+            lo = c * CHUNK + j * C
+            nc.scalar.copy(dx_sb[:, :, lo : lo + C], dx_ps[c][:, :, j * C : (j + 1) * C])
+
+        for c in range(CHUNKS):
+            new_g4(c)
+            for t in range(PACK):
+                gather_copy(c, t)
+            sigmoid(c)
+            gate_interleave(c, 2)
+            if c > 0:
+                quantize_g(c - 1)
+                mm1(2 * c - 2)
+                mm1(2 * c - 1)
+        silu(0)
+        quantize_g(3)
+        evac(0)
+        turn(0)
+        evac(1)
+        turn(1)
+        silu(1)
+        slope(0)
+        mm1(6)
+        mm1(7)
+        for c in range(CHUNKS):
+            if c + 2 < CHUNKS:
+                silu(c + 2)
+            for j in range(2):
+                e = 2 * c + j
+                times_slope(e)
+                if e > 0:
+                    quantize_da(e - 1)
+                    mm2(e - 1)
+                if e + 2 < E:
+                    evac(e + 2)
+                    turn(e + 2)
+                if j == 0 and c + 1 < CHUNKS:
+                    slope(c + 1)
+            if c > 0:
+                store_slots(c - 1)
+        quantize_da(7)
+        mm2(7)
+        store_slots(3)
+
+        for kt in range(2):
+            x1 = keep.tile([P, T], F32, name=f"x1_{kt}")
+            x2 = keep.tile([P, T], F32, name=f"x2_{kt}")
+            y = keep.tile([P, T], F32, name=f"y_{kt}")
+            nc.vector.tensor_copy(x1[:], dx_sb[:, kt, :].indirect(pos1_sb[:]))
+            nc.vector.tensor_copy(x2[:], dx_sb[:, kt, :].indirect(pos2_sb[:]))
+            adder = nc.gpsimd if kt == 0 else nc.vector
+            adder.tensor_tensor(out=y[:], in0=x1[:], in1=x2[:], op=ADD)
+            nc.sync.dma_start(out=out[kt * P : (kt + 1) * P, :], in_=y[:])

@@ -19,6 +19,7 @@ FP4X4 = mybir.dt.float4_e2m1fn_x4
 
 ADD, MULT, SUB = mybir.AluOpType.add, mybir.AluOpType.mult, mybir.AluOpType.subtract
 SIGMOID, SILU = mybir.ActivationFunctionType.Sigmoid, mybir.ActivationFunctionType.Silu
+IDENTITY = mybir.ActivationFunctionType.Identity
 
 P = 128
 PACK = 4
@@ -58,12 +59,14 @@ def tile_moe_bdx_mlp_silu_kernel(tc, dyT, a, w2_words, w2_scales, w1_words, w1_s
         for t in range(PACK):
             dy_t = keep.tile([P, T], F32, name=f"dy{t}")
             dy.append(dy_t)
-        a_sb, r_sb, s_sb, d_sb = [], [], [], []
+        a_sb, r_sb, s_sb, d_sb, u_sb = [], [], [], [], []
         for c in range(CHUNKS):
             a_c = keep.tile([P, PACK, CHUNK], F32, name=f"a{c}")
             r_c = keep.tile([P, PACK, CHUNK], F32, name=f"r{c}")
             s_c = keep.tile([P, PACK, CHUNK], F32, name=f"s{c}")
             d_c = keep.tile([P, PACK, CHUNK], F32, name=f"d{c}")
+            u_c = keep.tile([P, PACK, CHUNK], F32, name=f"u{c}")
+            u_sb.append(u_c)
             a_sb.append(a_c)
             r_sb.append(r_c)
             s_sb.append(s_c)
@@ -89,28 +92,30 @@ def tile_moe_bdx_mlp_silu_kernel(tc, dyT, a, w2_words, w2_scales, w1_words, w1_s
             for q in range(4):
                 nc.sync.dma_start(out=tile[q:P:32, :, :].bitcast(I32), in_=rows[q:16:4, :, :].bitcast(I32))
 
+        load_gate(1 * CHUNK, 2 * CHUNK)
         nc.sync.dma_start(offs_sb[:], offs)
-        load_dy(0)
-        load_dy(1)
+        load_gate(0 * CHUNK, 1 * CHUNK)
         load_dy(2)
         load_dy(3)
+        load_dy(0)
         load_a(0)
-        load_gate(0, 2 * CHUNK)
-        load_scales(w2s_sb, w2_scales)
-        load_words(w2_sb, w2_words, 0, 2)
-        load_a(1)
-        load_gate(2 * CHUNK, S)
         load_a(2)
-        load_words(w2_sb, w2_words, 2, 4)
-        load_a(3)
-        load_words(w2_sb, w2_words, 4, 8)
-        load_scales(w1s_sb, w1_scales)
-        load_words(w1_sb, w1_words, 0, 8)
+        load_dy(1)
+        load_gate(2 * CHUNK, 4 * CHUNK)
+        load_scales(w2s_sb, w2_scales)
         nc.sync.dma_start(pos1_sb[:], pos1)
         nc.sync.dma_start(pos2_sb[:], pos2)
+        load_a(1)
+        load_a(3)
+        load_words(w2_sb, w2_words, 4, 8)
+        load_words(w2_sb, w2_words, 2, 4)
+        load_words(w2_sb, w2_words, 0, 2)
+        load_words(w1_sb, w1_words, 0, 8)
+        load_scales(w1s_sb, w1_scales)
 
         dhT_ps, dhT_sb, dh_ps, dab, daq, das, dx_ps = {}, {}, {}, {}, {}, {}, {}
         g4, gb, gq, gs = {}, {}, {}, {}
+        negative = set()
         dx_sb = keep.tile([P, 2, S], F32, name="dx_sb")
 
         def cols(c):
@@ -137,6 +142,10 @@ def tile_moe_bdx_mlp_silu_kernel(tc, dyT, a, w2_words, w2_scales, w1_words, w1_s
             new_gb(c)
             nc.scalar.copy(gb[c][:], g4[c][:].rearrange("p t s -> p s t"))
 
+        def interleave_on_vector(c):
+            new_gb(c)
+            nc.vector.tensor_copy(gb[c][:], g4[c][:].rearrange("p t s -> p s t"))
+
         def gate_interleave(c, parts):
             new_gb(c)
             n = CHUNK // parts
@@ -158,14 +167,28 @@ def tile_moe_bdx_mlp_silu_kernel(tc, dyT, a, w2_words, w2_scales, w1_words, w1_s
         def sigmoid(c):
             nc.scalar.activation(r_sb[c][:], a_sb[c][:], SIGMOID)
 
+        zero = keep.tile([P, 1], F32, name="zero")
+
+        def tie(c):
+            nc.scalar.mul(zero[:], r_sb[c][:, 0, 0:1], 0.0)
+
         def silu(c):
-            nc.scalar.activation(s_sb[c][:], a_sb[c][:], SILU, scale=-1.0)
+            nc.scalar.activation(s_sb[c][:], a_sb[c][:], SILU, scale=-1.0, bias=zero[:])
 
         def silu_on_vector(c):
             nc.vector.scalar_tensor_tensor(out=s_sb[c][:], in0=r_sb[c][:], scalar=1.0, in1=a_sb[c][:], op0=SUB, op1=MULT)
 
         def slope(c):
+            negative.add(c)
             nc.vector.scalar_tensor_tensor(out=d_sb[c][:], in0=s_sb[c][:], scalar=1.0, in1=r_sb[c][:], op0=SUB, op1=MULT)
+
+        def rest(c):
+            nc.scalar.activation(u_sb[c][:], s_sb[c][:], IDENTITY, scale=-1.0, bias=1.0)
+
+        def slope_gpsimd(c, parts):
+            n = PACK // parts
+            for k in range(parts):
+                nc.gpsimd.tensor_tensor(out=d_sb[c][:, k * n : (k + 1) * n, :], in0=u_sb[c][:, k * n : (k + 1) * n, :], in1=r_sb[c][:, k * n : (k + 1) * n, :], op=MULT)
 
         def mm1(e):
             c, j = divmod(e, PER_CHUNK)
@@ -194,26 +217,33 @@ def tile_moe_bdx_mlp_silu_kernel(tc, dyT, a, w2_words, w2_scales, w1_words, w1_s
 
         def times_slope(e):
             c, j = divmod(e, PER_CHUNK)
-            tile = work.tile([P, C, PACK], BF16, name="dab", align_bytes=64)
+            if c not in dab:
+                tile = work.tile([P, CHUNK, PACK], BF16, name="dab", align_bytes=64)
+                dab[c] = tile
+            sign = -1.0 if c in negative else 1.0
             nc.vector.scalar_tensor_tensor(
-                out=tile[:],
+                out=dab[c][:, j * C : (j + 1) * C, :],
                 in0=dh_ps[e][:].rearrange("p t s -> p s t"),
-                scalar=-1.0,
+                scalar=sign,
                 in1=d_sb[c][:, :, j * C : (j + 1) * C].rearrange("p t s -> p s t"),
                 op0=MULT,
                 op1=MULT,
             )
-            dab[e] = tile
 
-        def quantize_da(e):
-            words = work.tile([P, C], U32, name="daq", align_bytes=64)
-            scales = work.tile([P, C], U8, name="das", align_bytes=64)
-            nc.vector.quantize_mx(out=words[:].bitcast(FP8X4), scales=scales[:], in_=dab[e][:].rearrange("p s t -> p (s t)"))
-            daq[e], das[e] = words, scales
+        def quantize_da(lo, hi):
+            c = lo // PER_CHUNK
+            j = lo % PER_CHUNK
+            n = (hi - lo) * C
+            words = work.tile([P, CHUNK], U32, name="daq", align_bytes=64)
+            scales = work.tile([P, CHUNK], U8, name="das", align_bytes=64)
+            nc.vector.quantize_mx(out=words[:, 0:n].bitcast(FP8X4), scales=scales[:, 0:n], in_=dab[c][:, j * C : j * C + n, :].rearrange("p s t -> p (s t)"))
+            for e in range(lo, hi):
+                daq[e] = words[:, (e - lo) * C : (e - lo + 1) * C]
+                das[e] = scales[:, (e - lo) * C : (e - lo + 1) * C]
 
         def mm2(e):
             c, j = divmod(e, PER_CHUNK)
-            if j == 0:
+            if c not in dx_ps:
                 tile = psum.tile([P, 2, CHUNK], F32, name="dx_ps", bufs=2)
                 dx_ps[c] = tile
             for kt in range(2):
@@ -221,8 +251,8 @@ def tile_moe_bdx_mlp_silu_kernel(tc, dyT, a, w2_words, w2_scales, w1_words, w1_s
                     out=dx_ps[c][:, kt, j * C : (j + 1) * C],
                     lhsT=w1_sb[:, e, kt * 2 * P : (kt + 1) * 2 * P].bitcast(FP4X4),
                     lhsT_scale=w1s_sb[:, e, kt * P : (kt + 1) * P],
-                    rhs=daq[e][:].bitcast(FP8X4),
-                    rhs_scale=das[e][:],
+                    rhs=daq[e].bitcast(FP8X4),
+                    rhs_scale=das[e],
                     start=True,
                     stop=True,
                 )
@@ -234,52 +264,119 @@ def tile_moe_bdx_mlp_silu_kernel(tc, dyT, a, w2_words, w2_scales, w1_words, w1_s
             lo = c * CHUNK + j * C
             nc.scalar.copy(dx_sb[:, :, lo : lo + C], dx_ps[c][:, :, j * C : (j + 1) * C])
 
-        for c in range(CHUNKS):
-            new_g4(c)
-            for t in range(PACK):
-                gather_copy(c, t)
-            sigmoid(c)
-            gate_interleave(c, 2)
-            if c > 0:
-                quantize_g(c - 1)
-                mm1(2 * c - 2)
-                mm1(2 * c - 1)
-        silu(0)
-        quantize_g(3)
-        evac(0)
-        turn(0)
-        evac(1)
-        turn(1)
-        silu(1)
-        slope(0)
-        mm1(6)
-        mm1(7)
-        for c in range(CHUNKS):
-            if c + 2 < CHUNKS:
-                silu(c + 2)
-            for j in range(2):
-                e = 2 * c + j
-                times_slope(e)
-                if e > 0:
-                    quantize_da(e - 1)
-                    mm2(e - 1)
-                if e + 2 < E:
-                    evac(e + 2)
-                    turn(e + 2)
-                if j == 0 and c + 1 < CHUNKS:
-                    slope(c + 1)
-            if c > 0:
-                store_slots(c - 1)
-        quantize_da(7)
-        mm2(7)
-        store_slots(3)
+        def store_slots_split(c, j):
+            lo = c * CHUNK + j * C
+            nc.vector.tensor_copy(dx_sb[:, 0, lo : lo + C], dx_ps[c][:, 0, j * C : (j + 1) * C])
+            nc.scalar.copy(dx_sb[:, 1, lo : lo + C], dx_ps[c][:, 1, j * C : (j + 1) * C])
 
+        new_g4(0)
+        gather_mul(0, 3)
+        new_g4(1)
+        gather_mul(1, 2)
+        gather_mul(0, 0)
+        gather_mul(0, 1)
+        sigmoid(3)
+        new_g4(2)
+        gather_mul(2, 0)
+        new_g4(3)
+        gather_mul(3, 2)
+        gather_mul(1, 0)
+        gather_mul(1, 1)
+        gather_mul(1, 3)
+        interleave(1)
+        gather_mul(3, 0)
+        tie(3)
+        silu(1)
+        gather_mul(2, 1)
+        quantize_g(1)
+        gather_mul(0, 2)
+        mm1(3)
+        gather_mul(2, 3)
+        gather_mul(3, 1)
+        sigmoid(1)
+        silu(0)
+        evac(3)
+        gather_mul(2, 2)
+        turn(3)
+        interleave(0)
+        mm1(2)
+        evac(2)
+        quantize_g(0)
+        sigmoid(0)
+        interleave_on_vector(2)
+        mm1(1)
+        gather_mul(3, 3)
+        silu(2)
+        evac(1)
+        quantize_g(2)
+        mm1(0)
+        mm1(4)
+        turn(1)
+        mm1(5)
+        slope(0)
+        slope(1)
+        evac(0)
+        turn(2)
+        sigmoid(2)
+        times_slope(1)
+        interleave_on_vector(3)
+        evac(4)
+        times_slope(2)
+        turn(0)
+        quantize_g(3)
+        mm1(6)
+        times_slope(3)
+        evac(5)
+        times_slope(0)
+        slope(2)
+        quantize_da(2, 4)
+        silu(3)
+        evac(6)
+        quantize_da(0, 2)
+        turn(4)
+        turn(6)
+        mm2(1)
+        mm2(2)
+        mm2(0)
+        mm1(7)
+        turn(5)
+        evac(7)
+        times_slope(5)
+        times_slope(4)
+        slope(3)
+        quantize_da(4, 6)
+        mm2(3)
+        mm2(4)
+        times_slope(6)
+        mm2(5)
+        turn(7)
+        times_slope(7)
+        store_slots(2)
+        quantize_da(6, 7)
+        quantize_da(7, 8)
+        mm2(6)
+        mm2(7)
+        store_slots_split(3, 1)
+        store_slots(1)
+        store_slots_part(3, 0)
+        store_slots(0)
+
+        HALF = T // 2
+        x1, x2, y = [], [], []
         for kt in range(2):
-            x1 = keep.tile([P, T], F32, name=f"x1_{kt}")
-            x2 = keep.tile([P, T], F32, name=f"x2_{kt}")
-            y = keep.tile([P, T], F32, name=f"y_{kt}")
-            nc.vector.tensor_copy(x1[:], dx_sb[:, kt, :].indirect(pos1_sb[:]))
-            nc.vector.tensor_copy(x2[:], dx_sb[:, kt, :].indirect(pos2_sb[:]))
-            adder = nc.gpsimd if kt == 0 else nc.vector
-            adder.tensor_tensor(out=y[:], in0=x1[:], in1=x2[:], op=ADD)
-            nc.sync.dma_start(out=out[kt * P : (kt + 1) * P, :], in_=y[:])
+            x1_k = keep.tile([P, T], F32, name=f"x1_{kt}")
+            x2_k = keep.tile([P, T], F32, name=f"x2_{kt}")
+            y_k = keep.tile([P, T], F32, name=f"y_{kt}")
+            x1.append(x1_k)
+            x2.append(x2_k)
+            y.append(y_k)
+        nc.vector.tensor_copy(x1[0][:], dx_sb[:, 0, :].indirect(pos1_sb[:]))
+        nc.vector.tensor_copy(x2[0][:], dx_sb[:, 0, :].indirect(pos2_sb[:]))
+        nc.gpsimd.tensor_tensor(out=y[0][:], in0=x1[0][:], in1=x2[0][:], op=ADD)
+        nc.sync.dma_start(out=out[0:P, :], in_=y[0][:])
+        nc.vector.tensor_copy(x1[1][:], dx_sb[:, 1, :].indirect(pos1_sb[:]))
+        for h in range(2):
+            tok = slice(h * HALF, (h + 1) * HALF)
+            nc.vector.tensor_copy(x2[1][:, tok], dx_sb[:, 1, :].indirect(pos2_sb[:, h * HALF // 16 : (h + 1) * HALF // 16]))
+            nc.vector.tensor_tensor(out=y[1][:, tok], in0=x1[1][:, tok], in1=x2[1][:, tok], op=ADD)
+            nc.sync.dma_start(out=out[P : 2 * P, tok], in_=y[1][:, tok])

@@ -19,11 +19,12 @@ FP4X4 = mybir.dt.float4_e2m1fn_x4
 
 ADD, MULT, SUB = mybir.AluOpType.add, mybir.AluOpType.mult, mybir.AluOpType.subtract
 SIGMOID, SILU = mybir.ActivationFunctionType.Sigmoid, mybir.ActivationFunctionType.Silu
-IDENTITY = mybir.ActivationFunctionType.Identity
 
 P = 128
 PACK = 4
 CHUNK = 256
+RUN = 512
+PAD = 32
 CHUNKS = S // CHUNK
 PER_CHUNK = CHUNK // C
 
@@ -57,29 +58,31 @@ def tile_moe_bdx_mlp_silu_kernel(tc, dyT, a, w2_words, w2_scales, w1_words, w1_s
         gate_sb = keep.tile([P, S], F32, name="gate_sb")
         dy = []
         for t in range(PACK):
-            dy_t = keep.tile([P, T], F32, name=f"dy{t}")
+            dy_t = keep.tile([P, T + PAD], F32, name=f"dy{t}")
             dy.append(dy_t)
-        a_sb, r_sb, s_sb, d_sb, u_sb = [], [], [], [], []
+        a_sb, r_sb, s_sb, d_sb = [], [], [], []
         for c in range(CHUNKS):
             a_c = keep.tile([P, PACK, CHUNK], F32, name=f"a{c}")
             r_c = keep.tile([P, PACK, CHUNK], F32, name=f"r{c}")
             s_c = keep.tile([P, PACK, CHUNK], F32, name=f"s{c}")
             d_c = keep.tile([P, PACK, CHUNK], F32, name=f"d{c}")
-            u_c = keep.tile([P, PACK, CHUNK], F32, name=f"u{c}")
-            u_sb.append(u_c)
             a_sb.append(a_c)
             r_sb.append(r_c)
             s_sb.append(s_c)
             d_sb.append(d_c)
 
-        dy_hbm = dyT.rearrange("(p t) s -> p t s", t=PACK)
+        dy_hbm = dyT.rearrange("(p t) s -> p (t s)", t=PACK)
         a_hbm = a.rearrange("(p t) s -> p t s", t=PACK)
 
         def load_gate(lo, hi):
             nc.sync.dma_start(out=gate_sb[:, lo:hi], in_=gate[0:P, lo:hi])
 
         def load_dy(t):
-            nc.sync.dma_start(out=dy[t][:], in_=dy_hbm[:, t, :])
+            if t < PACK - 1:
+                nc.sync.dma_start(out=dy[t][:], in_=dy_hbm[:, t * T : (t + 1) * T + PAD])
+            else:
+                nc.sync.dma_start(out=dy[t][:, 0:T], in_=dy_hbm[:, t * T : (t + 1) * T])
+                nc.sync.dma_start(out=dy[t][:, T : T + PAD], in_=dy_hbm[:, 0:PAD])
 
         def load_a(c):
             nc.sync.dma_start(out=a_sb[c][:], in_=a_hbm[:, :, c * CHUNK : (c + 1) * CHUNK])
@@ -92,47 +95,47 @@ def tile_moe_bdx_mlp_silu_kernel(tc, dyT, a, w2_words, w2_scales, w1_words, w1_s
             for q in range(4):
                 nc.sync.dma_start(out=tile[q:P:32, :, :].bitcast(I32), in_=rows[q:16:4, :, :].bitcast(I32))
 
-        load_gate(1 * CHUNK, 2 * CHUNK)
         nc.sync.dma_start(offs_sb[:], offs)
+        load_gate(1 * CHUNK, 2 * CHUNK)
         load_gate(0 * CHUNK, 1 * CHUNK)
         load_dy(2)
         load_dy(3)
+        load_a(1)
         load_dy(0)
-        load_a(0)
         load_a(2)
         load_dy(1)
         load_gate(2 * CHUNK, 4 * CHUNK)
-        load_scales(w2s_sb, w2_scales)
-        nc.sync.dma_start(pos1_sb[:], pos1)
-        nc.sync.dma_start(pos2_sb[:], pos2)
-        load_a(1)
-        load_a(3)
+        load_a(0)
         load_words(w2_sb, w2_words, 4, 8)
         load_words(w2_sb, w2_words, 2, 4)
+        load_a(3)
         load_words(w2_sb, w2_words, 0, 2)
-        load_words(w1_sb, w1_words, 0, 8)
+        nc.sync.dma_start(pos1_sb[:], pos1)
+        nc.sync.dma_start(pos2_sb[:], pos2)
+        load_scales(w2s_sb, w2_scales)
         load_scales(w1s_sb, w1_scales)
+        load_words(w1_sb, w1_words, 0, 8)
 
         dhT_ps, dhT_sb, dh_ps, dab, daq, das, dx_ps = {}, {}, {}, {}, {}, {}, {}
         g4, gb, gq, gs = {}, {}, {}, {}
-        negative = set()
         dx_sb = keep.tile([P, 2, S], F32, name="dx_sb")
 
         def cols(c):
             return slice(c * CHUNK, (c + 1) * CHUNK)
 
-        def idx(c):
-            return offs_sb[:, c * CHUNK // 16 : (c + 1) * CHUNK // 16]
+        def g4_of(c):
+            return g4[c // 2][:, :, (c % 2) * CHUNK : (c % 2 + 1) * CHUNK]
 
-        def new_g4(c):
-            tile = work.tile([P, PACK, CHUNK], F32, name="g4")
-            g4[c] = tile
-
-        def gather_copy(c, t):
-            nc.vector.tensor_copy(g4[c][:, t, :], dy[t][:].indirect(idx(c)))
-
-        def gather_mul(c, t):
-            nc.vector.tensor_tensor(out=g4[c][:, t, :], in0=dy[t][:].indirect(idx(c)), in1=gate_sb[:, cols(c)], op=MULT)
+        def gather(h, t):
+            if h not in g4:
+                tile = work.tile([P, PACK, RUN], F32, name="g4", bufs=2)
+                g4[h] = tile
+            nc.vector.tensor_tensor(
+                out=g4[h][:, t, :],
+                in0=dy[t][:].indirect(offs_sb[:, h * RUN // 16 : (h + 1) * RUN // 16]),
+                in1=gate_sb[:, h * RUN : (h + 1) * RUN],
+                op=MULT,
+            )
 
         def new_gb(c):
             tile = work.tile([P, CHUNK, PACK], BF16, name="gb", align_bytes=64)
@@ -140,23 +143,11 @@ def tile_moe_bdx_mlp_silu_kernel(tc, dyT, a, w2_words, w2_scales, w1_words, w1_s
 
         def interleave(c):
             new_gb(c)
-            nc.scalar.copy(gb[c][:], g4[c][:].rearrange("p t s -> p s t"))
+            nc.scalar.copy(gb[c][:].rearrange("p (c i) t -> p c t i", i=4), g4_of(c).rearrange("p t (c i) -> p c t i", i=4))
 
         def interleave_on_vector(c):
             new_gb(c)
-            nc.vector.tensor_copy(gb[c][:], g4[c][:].rearrange("p t s -> p s t"))
-
-        def gate_interleave(c, parts):
-            new_gb(c)
-            n = CHUNK // parts
-            for k in range(parts):
-                lo = k * n
-                nc.gpsimd.tensor_tensor(
-                    out=gb[c][:, lo : lo + n, :],
-                    in0=g4[c][:, :, lo : lo + n].rearrange("p t s -> p s t"),
-                    in1=gate_sb[:, c * CHUNK + lo : c * CHUNK + lo + n].unsqueeze(2).to_broadcast([P, n, PACK]),
-                    op=MULT,
-                )
+            nc.vector.tensor_copy(gb[c][:].rearrange("p (c i) t -> p c t i", i=4), g4_of(c).rearrange("p t (c i) -> p c t i", i=4))
 
         def quantize_g(c):
             words = work.tile([P, CHUNK], U32, name="gq", align_bytes=64)
@@ -179,16 +170,7 @@ def tile_moe_bdx_mlp_silu_kernel(tc, dyT, a, w2_words, w2_scales, w1_words, w1_s
             nc.vector.scalar_tensor_tensor(out=s_sb[c][:], in0=r_sb[c][:], scalar=1.0, in1=a_sb[c][:], op0=SUB, op1=MULT)
 
         def slope(c):
-            negative.add(c)
             nc.vector.scalar_tensor_tensor(out=d_sb[c][:], in0=s_sb[c][:], scalar=1.0, in1=r_sb[c][:], op0=SUB, op1=MULT)
-
-        def rest(c):
-            nc.scalar.activation(u_sb[c][:], s_sb[c][:], IDENTITY, scale=-1.0, bias=1.0)
-
-        def slope_gpsimd(c, parts):
-            n = PACK // parts
-            for k in range(parts):
-                nc.gpsimd.tensor_tensor(out=d_sb[c][:, k * n : (k + 1) * n, :], in0=u_sb[c][:, k * n : (k + 1) * n, :], in1=r_sb[c][:, k * n : (k + 1) * n, :], op=MULT)
 
         def mm1(e):
             c, j = divmod(e, PER_CHUNK)
@@ -209,6 +191,11 @@ def tile_moe_bdx_mlp_silu_kernel(tc, dyT, a, w2_words, w2_scales, w1_words, w1_s
             nc.scalar.copy(tile[:], dhT_ps[e][:].rearrange("s (m t) -> s t m", t=PACK))
             dhT_sb[e] = tile
 
+        def evac_v(e):
+            tile = work.tile([P, PACK, P], F32, name="dhT", bufs=4)
+            nc.vector.tensor_copy(tile[:], dhT_ps[e][:].rearrange("s (m t) -> s t m", t=PACK))
+            dhT_sb[e] = tile
+
         def turn(e):
             tile = psum.tile([P, PACK, C], F32, name="dh_ps", bufs=3)
             for t in range(PACK):
@@ -220,14 +207,11 @@ def tile_moe_bdx_mlp_silu_kernel(tc, dyT, a, w2_words, w2_scales, w1_words, w1_s
             if c not in dab:
                 tile = work.tile([P, CHUNK, PACK], BF16, name="dab", align_bytes=64)
                 dab[c] = tile
-            sign = -1.0 if c in negative else 1.0
-            nc.vector.scalar_tensor_tensor(
-                out=dab[c][:, j * C : (j + 1) * C, :],
-                in0=dh_ps[e][:].rearrange("p t s -> p s t"),
-                scalar=sign,
-                in1=d_sb[c][:, :, j * C : (j + 1) * C].rearrange("p t s -> p s t"),
-                op0=MULT,
-                op1=MULT,
+            nc.vector.tensor_tensor(
+                out=dab[c][:, j * C : (j + 1) * C, :].rearrange("p (c i) t -> p c t i", i=4),
+                in0=dh_ps[e][:].rearrange("p t (c i) -> p c t i", i=4),
+                in1=d_sb[c][:, :, j * C : (j + 1) * C].rearrange("p t (c i) -> p c t i", i=4),
+                op=MULT,
             )
 
         def quantize_da(lo, hi):
@@ -258,108 +242,96 @@ def tile_moe_bdx_mlp_silu_kernel(tc, dyT, a, w2_words, w2_scales, w1_words, w1_s
                 )
 
         def store_slots(c):
-            nc.scalar.copy(dx_sb[:, :, cols(c)], dx_ps[c][:])
+            nc.scalar.mul(dx_sb[:, :, cols(c)], dx_ps[c][:], -1.0)
 
         def store_slots_part(c, j):
             lo = c * CHUNK + j * C
-            nc.scalar.copy(dx_sb[:, :, lo : lo + C], dx_ps[c][:, :, j * C : (j + 1) * C])
+            nc.scalar.mul(dx_sb[:, :, lo : lo + C], dx_ps[c][:, :, j * C : (j + 1) * C], -1.0)
 
         def store_slots_split(c, j):
             lo = c * CHUNK + j * C
-            nc.vector.tensor_copy(dx_sb[:, 0, lo : lo + C], dx_ps[c][:, 0, j * C : (j + 1) * C])
-            nc.scalar.copy(dx_sb[:, 1, lo : lo + C], dx_ps[c][:, 1, j * C : (j + 1) * C])
+            nc.vector.tensor_scalar_mul(dx_sb[:, 0, lo : lo + C], dx_ps[c][:, 0, j * C : (j + 1) * C], -1.0)
+            nc.scalar.mul(dx_sb[:, 1, lo : lo + C], dx_ps[c][:, 1, j * C : (j + 1) * C], -1.0)
 
-        new_g4(0)
-        gather_mul(0, 3)
-        new_g4(1)
-        gather_mul(1, 2)
-        gather_mul(0, 0)
-        gather_mul(0, 1)
-        sigmoid(3)
-        new_g4(2)
-        gather_mul(2, 0)
-        new_g4(3)
-        gather_mul(3, 2)
-        gather_mul(1, 0)
-        gather_mul(1, 1)
-        gather_mul(1, 3)
-        interleave(1)
-        gather_mul(3, 0)
-        tie(3)
-        silu(1)
-        gather_mul(2, 1)
-        quantize_g(1)
-        gather_mul(0, 2)
-        mm1(3)
-        gather_mul(2, 3)
-        gather_mul(3, 1)
+        gather(0, 3)
+        gather(1, 0)
         sigmoid(1)
-        silu(0)
-        evac(3)
-        gather_mul(2, 2)
-        turn(3)
+        sigmoid(3)
+        gather(0, 2)
+        sigmoid(2)
+        gather(1, 1)
+        gather(0, 0)
+        gather(0, 1)
+        interleave(1)
         interleave(0)
+        quantize_g(1)
         mm1(2)
-        evac(2)
+        tie(3)
+        gather(1, 2)
         quantize_g(0)
         sigmoid(0)
-        interleave_on_vector(2)
-        mm1(1)
-        gather_mul(3, 3)
-        silu(2)
-        evac(1)
-        quantize_g(2)
+        silu(0)
         mm1(0)
-        mm1(4)
-        turn(1)
-        mm1(5)
-        slope(0)
-        slope(1)
-        evac(0)
-        turn(2)
-        sigmoid(2)
-        times_slope(1)
-        interleave_on_vector(3)
-        evac(4)
-        times_slope(2)
+        mm1(3)
+        mm1(1)
+        evac(3)
+        evac(2)
+        evac_v(0)
+        silu(1)
         turn(0)
-        quantize_g(3)
-        mm1(6)
+        turn(3)
+        slope(1)
         times_slope(3)
-        evac(5)
+        gather(1, 3)
+        silu(2)
+        interleave_on_vector(2)
+        evac(1)
+        interleave_on_vector(3)
+        quantize_g(2)
+        mm1(4)
+        quantize_g(3)
+        evac(4)
+        slope(0)
+        mm1(5)
+        turn(1)
+        mm1(6)
         times_slope(0)
+        evac(5)
         slope(2)
-        quantize_da(2, 4)
-        silu(3)
-        evac(6)
-        quantize_da(0, 2)
-        turn(4)
-        turn(6)
-        mm2(1)
-        mm2(2)
-        mm2(0)
+        times_slope(1)
         mm1(7)
+        quantize_da(0, 2)
+        turn(2)
+        times_slope(2)
+        turn(4)
+        silu(3)
         turn(5)
-        evac(7)
-        times_slope(5)
-        times_slope(4)
+        evac(6)
+        turn(6)
         slope(3)
-        quantize_da(4, 6)
-        mm2(3)
-        mm2(4)
+        mm2(0)
+        times_slope(4)
+        quantize_da(2, 4)
+        times_slope(5)
         times_slope(6)
-        mm2(5)
+        quantize_da(4, 6)
+        mm2(1)
+        evac(7)
         turn(7)
-        times_slope(7)
-        store_slots(2)
         quantize_da(6, 7)
+        mm2(3)
+        times_slope(7)
+        mm2(5)
         quantize_da(7, 8)
+        mm2(2)
+        mm2(4)
         mm2(6)
-        mm2(7)
-        store_slots_split(3, 1)
-        store_slots(1)
-        store_slots_part(3, 0)
         store_slots(0)
+        store_slots(1)
+        mm2(7)
+        store_slots_part(3, 0)
+        store_slots_split(3, 1)
+        store_slots(2)
 
         HALF = T // 2
         x1, x2, y = [], [], []

@@ -60,14 +60,12 @@ def tile_moe_bdx_mlp_silu_kernel(tc, dyT, a, w2_words, w2_scales, w1_words, w1_s
         for t in range(PACK):
             dy_t = keep.tile([P, T + PAD], F32, name=f"dy{t}")
             dy.append(dy_t)
-        a_sb, r_sb, s_sb, d_sb = [], [], [], []
+        a_sb = keep.tile([P, PACK, S], F32, name="a_sb")
+        r_sb = keep.tile([P, PACK, S], F32, name="r_sb")
+        s_sb, d_sb = [], []
         for c in range(CHUNKS):
-            a_c = keep.tile([P, PACK, CHUNK], F32, name=f"a{c}")
-            r_c = keep.tile([P, PACK, CHUNK], F32, name=f"r{c}")
             s_c = keep.tile([P, PACK, CHUNK], F32, name=f"s{c}")
             d_c = keep.tile([P, PACK, CHUNK], F32, name=f"d{c}")
-            a_sb.append(a_c)
-            r_sb.append(r_c)
             s_sb.append(s_c)
             d_sb.append(d_c)
 
@@ -84,8 +82,8 @@ def tile_moe_bdx_mlp_silu_kernel(tc, dyT, a, w2_words, w2_scales, w1_words, w1_s
                 nc.sync.dma_start(out=dy[t][:, 0:T], in_=dy_hbm[:, t * T : (t + 1) * T])
                 nc.sync.dma_start(out=dy[t][:, T : T + PAD], in_=dy_hbm[:, 0:PAD])
 
-        def load_a(c):
-            nc.sync.dma_start(out=a_sb[c][:], in_=a_hbm[:, :, c * CHUNK : (c + 1) * CHUNK])
+        def load_a(t, lo, hi):
+            nc.sync.dma_start(out=a_sb[:, t, lo:hi], in_=a_hbm[:, t, lo:hi])
 
         def load_words(tile, words, lo, hi):
             nc.sync.dma_start(out=tile[:, lo:hi, :].bitcast(I32), in_=words.rearrange("e s p c -> p (e s) c")[:, lo:hi, :].bitcast(I32))
@@ -95,26 +93,27 @@ def tile_moe_bdx_mlp_silu_kernel(tc, dyT, a, w2_words, w2_scales, w1_words, w1_s
             for q in range(4):
                 nc.sync.dma_start(out=tile[q:P:32, :, :].bitcast(I32), in_=rows[q:16:4, :, :].bitcast(I32))
 
-        nc.sync.dma_start(offs_sb[:], offs)
-        load_gate(1 * CHUNK, 2 * CHUNK)
         load_gate(0 * CHUNK, 1 * CHUNK)
-        load_dy(2)
-        load_dy(3)
-        load_a(1)
+        nc.sync.dma_start(offs_sb[:], offs)
         load_dy(0)
-        load_a(2)
+        load_gate(1 * CHUNK, 2 * CHUNK)
+        load_dy(2)
         load_dy(1)
-        load_gate(2 * CHUNK, 4 * CHUNK)
-        load_a(0)
-        load_words(w2_sb, w2_words, 4, 8)
-        load_words(w2_sb, w2_words, 2, 4)
-        load_a(3)
-        load_words(w2_sb, w2_words, 0, 2)
+        load_a(2, 0, S)
+        load_dy(3)
         nc.sync.dma_start(pos1_sb[:], pos1)
         nc.sync.dma_start(pos2_sb[:], pos2)
+        load_a(0, 1 * RUN, 2 * RUN)
+        load_gate(2 * CHUNK, 4 * CHUNK)
+        load_a(0, 0 * RUN, 1 * RUN)
+        load_a(1, 0, S)
+        load_a(3, 0, S)
         load_scales(w2s_sb, w2_scales)
-        load_scales(w1s_sb, w1_scales)
+        load_words(w2_sb, w2_words, 0, 2)
+        load_words(w2_sb, w2_words, 2, 4)
+        load_words(w2_sb, w2_words, 4, 8)
         load_words(w1_sb, w1_words, 0, 8)
+        load_scales(w1s_sb, w1_scales)
 
         dhT_ps, dhT_sb, dh_ps, dab, daq, das, dx_ps = {}, {}, {}, {}, {}, {}, {}
         g4, gb, gq, gs = {}, {}, {}, {}
@@ -126,14 +125,14 @@ def tile_moe_bdx_mlp_silu_kernel(tc, dyT, a, w2_words, w2_scales, w1_words, w1_s
         def g4_of(c):
             return g4[c // 2][:, :, (c % 2) * CHUNK : (c % 2 + 1) * CHUNK]
 
-        def gather(h, t):
+        def gather(h, t, lo=0, hi=RUN):
             if h not in g4:
                 tile = work.tile([P, PACK, RUN], F32, name="g4", bufs=2)
                 g4[h] = tile
             nc.vector.tensor_tensor(
-                out=g4[h][:, t, :],
-                in0=dy[t][:].indirect(offs_sb[:, h * RUN // 16 : (h + 1) * RUN // 16]),
-                in1=gate_sb[:, h * RUN : (h + 1) * RUN],
+                out=g4[h][:, t, lo:hi],
+                in0=dy[t][:].indirect(offs_sb[:, (h * RUN + lo) // 16 : (h * RUN + hi) // 16]),
+                in1=gate_sb[:, h * RUN + lo : h * RUN + hi],
                 op=MULT,
             )
 
@@ -155,22 +154,19 @@ def tile_moe_bdx_mlp_silu_kernel(tc, dyT, a, w2_words, w2_scales, w1_words, w1_s
             nc.vector.quantize_mx(out=words[:].bitcast(FP8X4), scales=scales[:], in_=gb[c][:].rearrange("p s t -> p (s t)"))
             gq[c], gs[c] = words, scales
 
-        def sigmoid(c):
-            nc.scalar.activation(r_sb[c][:], a_sb[c][:], SIGMOID)
+        def sigmoid(t, lo, hi):
+            nc.scalar.activation(r_sb[:, t, lo:hi], a_sb[:, t, lo:hi], SIGMOID)
 
         zero = keep.tile([P, 1], F32, name="zero")
 
-        def tie(c):
-            nc.scalar.mul(zero[:], r_sb[c][:, 0, 0:1], 0.0)
+        def tie(t):
+            nc.scalar.mul(zero[:], r_sb[:, t, S - 1 : S], 0.0)
 
         def silu(c):
-            nc.scalar.activation(s_sb[c][:], a_sb[c][:], SILU, scale=-1.0, bias=zero[:])
-
-        def silu_on_vector(c):
-            nc.vector.scalar_tensor_tensor(out=s_sb[c][:], in0=r_sb[c][:], scalar=1.0, in1=a_sb[c][:], op0=SUB, op1=MULT)
+            nc.scalar.activation(s_sb[c][:], a_sb[:, :, cols(c)], SILU, scale=-1.0, bias=zero[:])
 
         def slope(c):
-            nc.vector.scalar_tensor_tensor(out=d_sb[c][:], in0=s_sb[c][:], scalar=1.0, in1=r_sb[c][:], op0=SUB, op1=MULT)
+            nc.vector.scalar_tensor_tensor(out=d_sb[c][:], in0=s_sb[c][:], scalar=1.0, in1=r_sb[:, :, cols(c)], op0=SUB, op1=MULT)
 
         def mm1(e):
             c, j = divmod(e, PER_CHUNK)
@@ -189,11 +185,6 @@ def tile_moe_bdx_mlp_silu_kernel(tc, dyT, a, w2_words, w2_scales, w1_words, w1_s
         def evac(e):
             tile = work.tile([P, PACK, P], F32, name="dhT", bufs=4)
             nc.scalar.copy(tile[:], dhT_ps[e][:].rearrange("s (m t) -> s t m", t=PACK))
-            dhT_sb[e] = tile
-
-        def evac_v(e):
-            tile = work.tile([P, PACK, P], F32, name="dhT", bufs=4)
-            nc.vector.tensor_copy(tile[:], dhT_ps[e][:].rearrange("s (m t) -> s t m", t=PACK))
             dhT_sb[e] = tile
 
         def turn(e):
@@ -253,85 +244,87 @@ def tile_moe_bdx_mlp_silu_kernel(tc, dyT, a, w2_words, w2_scales, w1_words, w1_s
             nc.vector.tensor_scalar_mul(dx_sb[:, 0, lo : lo + C], dx_ps[c][:, 0, j * C : (j + 1) * C], -1.0)
             nc.scalar.mul(dx_sb[:, 1, lo : lo + C], dx_ps[c][:, 1, j * C : (j + 1) * C], -1.0)
 
-        gather(0, 3)
-        gather(1, 0)
-        sigmoid(1)
-        sigmoid(3)
-        gather(0, 2)
-        sigmoid(2)
-        gather(1, 1)
-        gather(0, 0)
-        gather(0, 1)
-        interleave(1)
-        interleave(0)
-        quantize_g(1)
-        mm1(2)
-        tie(3)
+        gather(0, 0, 1 * CHUNK, 2 * CHUNK)
         gather(1, 2)
+        gather(0, 0, 0 * CHUNK, 1 * CHUNK)
+        gather(1, 1)
+        gather(1, 3)
+        gather(0, 2)
+        sigmoid(0, 0 * RUN, 1 * RUN)
+        sigmoid(0, 1 * RUN, 2 * RUN)
+        gather(0, 1)
+        gather(0, 3)
+        interleave_on_vector(0)
+        sigmoid(3, 0, S)
+        sigmoid(2, 0, S)
+        tie(3)
+        gather(1, 0)
+        interleave_on_vector(3)
+        interleave(1)
+        interleave_on_vector(2)
         quantize_g(0)
-        sigmoid(0)
         silu(0)
-        mm1(0)
-        mm1(3)
+        quantize_g(1)
+        quantize_g(3)
         mm1(1)
-        evac(3)
-        evac(2)
-        evac_v(0)
+        evac(1)
+        mm1(0)
+        quantize_g(2)
+        mm1(3)
+        mm1(2)
         silu(1)
+        mm1(4)
+        evac(0)
+        sigmoid(1, 0, S)
+        turn(1)
+        slope(0)
         turn(0)
+        mm1(5)
+        evac(3)
+        silu(2)
+        evac(2)
+        evac(4)
         turn(3)
+        silu(3)
+        turn(2)
+        times_slope(1)
         slope(1)
         times_slope(3)
-        gather(1, 3)
-        silu(2)
-        interleave_on_vector(2)
-        evac(1)
-        interleave_on_vector(3)
-        quantize_g(2)
-        mm1(4)
-        quantize_g(3)
-        evac(4)
-        slope(0)
-        mm1(5)
-        turn(1)
-        mm1(6)
-        times_slope(0)
-        evac(5)
-        slope(2)
-        times_slope(1)
-        mm1(7)
-        quantize_da(0, 2)
-        turn(2)
-        times_slope(2)
         turn(4)
-        silu(3)
-        turn(5)
-        evac(6)
-        turn(6)
-        slope(3)
-        mm2(0)
-        times_slope(4)
-        quantize_da(2, 4)
-        times_slope(5)
-        times_slope(6)
-        quantize_da(4, 6)
+        evac(5)
+        times_slope(2)
+        times_slope(0)
+        mm1(6)
+        quantize_da(0, 2)
         mm2(1)
+        mm1(7)
+        evac(6)
+        turn(5)
+        slope(2)
+        quantize_da(2, 4)
+        times_slope(4)
+        times_slope(5)
+        turn(6)
+        quantize_da(4, 6)
         evac(7)
         turn(7)
-        quantize_da(6, 7)
+        slope(3)
+        mm2(0)
+        store_slots(0)
         mm2(3)
+        times_slope(6)
         times_slope(7)
-        mm2(5)
+        quantize_da(6, 7)
+        mm2(4)
         quantize_da(7, 8)
         mm2(2)
-        mm2(4)
+        mm2(5)
         mm2(6)
-        store_slots(0)
-        store_slots(1)
-        mm2(7)
         store_slots_part(3, 0)
-        store_slots_split(3, 1)
+        mm2(7)
         store_slots(2)
+        store_slots_split(3, 1)
+        store_slots(1)
 
         HALF = T // 2
         x1, x2, y = [], [], []
@@ -350,5 +343,6 @@ def tile_moe_bdx_mlp_silu_kernel(tc, dyT, a, w2_words, w2_scales, w1_words, w1_s
         for h in range(2):
             tok = slice(h * HALF, (h + 1) * HALF)
             nc.vector.tensor_copy(x2[1][:, tok], dx_sb[:, 1, :].indirect(pos2_sb[:, h * HALF // 16 : (h + 1) * HALF // 16]))
-            nc.vector.tensor_tensor(out=y[1][:, tok], in0=x1[1][:, tok], in1=x2[1][:, tok], op=ADD)
+            adder = nc.gpsimd if h == 0 else nc.vector
+            adder.tensor_tensor(out=y[1][:, tok], in0=x1[1][:, tok], in1=x2[1][:, tok], op=ADD)
             nc.sync.dma_start(out=out[P : 2 * P, tok], in_=y[1][:, tok])

@@ -94,25 +94,25 @@ def tile_moe_bdx_mlp_silu_kernel(tc, dyT, a, w2_words, w2_scales, w1_words, w1_s
                 nc.sync.dma_start(out=tile[q:P:32, :, :].bitcast(I32), in_=rows[q:16:4, :, :].bitcast(I32))
 
         load_gate(0 * CHUNK, 1 * CHUNK)
-        nc.sync.dma_start(offs_sb[:], offs)
         load_dy(0)
+        nc.sync.dma_start(offs_sb[:], offs)
+        load_gate(2 * CHUNK, 4 * CHUNK)
         load_gate(1 * CHUNK, 2 * CHUNK)
+        load_dy(3)
+        load_a(0, 1 * RUN, 2 * RUN)
         load_dy(2)
+        load_a(0, 0 * RUN, 1 * RUN)
+        load_a(3, 0, S)
+        load_a(1, 0, S)
         load_dy(1)
         load_a(2, 0, S)
-        load_dy(3)
-        nc.sync.dma_start(pos1_sb[:], pos1)
-        nc.sync.dma_start(pos2_sb[:], pos2)
-        load_a(0, 1 * RUN, 2 * RUN)
-        load_gate(2 * CHUNK, 4 * CHUNK)
-        load_a(0, 0 * RUN, 1 * RUN)
-        load_a(1, 0, S)
-        load_a(3, 0, S)
         load_scales(w2s_sb, w2_scales)
         load_words(w2_sb, w2_words, 0, 2)
         load_words(w2_sb, w2_words, 2, 4)
         load_words(w2_sb, w2_words, 4, 8)
         load_words(w1_sb, w1_words, 0, 8)
+        nc.sync.dma_start(pos1_sb[:], pos1)
+        nc.sync.dma_start(pos2_sb[:], pos2)
         load_scales(w1s_sb, w1_scales)
 
         dhT_ps, dhT_sb, dh_ps, dab, daq, das, dx_ps = {}, {}, {}, {}, {}, {}, {}
@@ -244,87 +244,88 @@ def tile_moe_bdx_mlp_silu_kernel(tc, dyT, a, w2_words, w2_scales, w1_words, w1_s
             nc.vector.tensor_scalar_mul(dx_sb[:, 0, lo : lo + C], dx_ps[c][:, 0, j * C : (j + 1) * C], -1.0)
             nc.scalar.mul(dx_sb[:, 1, lo : lo + C], dx_ps[c][:, 1, j * C : (j + 1) * C], -1.0)
 
-        gather(0, 0, 1 * CHUNK, 2 * CHUNK)
-        gather(1, 2)
         gather(0, 0, 0 * CHUNK, 1 * CHUNK)
-        gather(1, 1)
-        gather(1, 3)
-        gather(0, 2)
-        sigmoid(0, 0 * RUN, 1 * RUN)
-        sigmoid(0, 1 * RUN, 2 * RUN)
-        gather(0, 1)
-        gather(0, 3)
-        interleave_on_vector(0)
-        sigmoid(3, 0, S)
-        sigmoid(2, 0, S)
-        tie(3)
         gather(1, 0)
-        interleave_on_vector(3)
-        interleave(1)
-        interleave_on_vector(2)
-        quantize_g(0)
-        silu(0)
-        quantize_g(1)
-        quantize_g(3)
-        mm1(1)
-        evac(1)
-        mm1(0)
-        quantize_g(2)
-        mm1(3)
-        mm1(2)
-        silu(1)
-        mm1(4)
-        evac(0)
+        gather(1, 3)
+        sigmoid(0, 1 * RUN, 2 * RUN)
+        gather(1, 2)
+        sigmoid(0, 0 * RUN, 1 * RUN)
+        gather(0, 2)
+        sigmoid(3, 0, S)
+        gather(0, 3)
         sigmoid(1, 0, S)
-        turn(1)
+        gather(0, 1)
+        tie(3)
+        sigmoid(2, 0, S)
+        gather(0, 0, 1 * CHUNK, 2 * CHUNK)
+        silu(0)
+        interleave_on_vector(0)
+        interleave_on_vector(1)
+        quantize_g(0)
+        gather(1, 1)
+        mm1(1)
+        mm1(0)
+        silu(1)
+        quantize_g(1)
+        interleave_on_vector(2)
+        mm1(3)
+        interleave_on_vector(3)
+        evac(1)
+        quantize_g(2)
+        evac(0)
+        mm1(2)
         slope(0)
-        turn(0)
-        mm1(5)
+        turn(1)
         evac(3)
-        silu(2)
-        evac(2)
-        evac(4)
-        turn(3)
+        turn(0)
         silu(3)
-        turn(2)
-        times_slope(1)
         slope(1)
-        times_slope(3)
-        turn(4)
-        evac(5)
-        times_slope(2)
-        times_slope(0)
-        mm1(6)
-        quantize_da(0, 2)
-        mm2(1)
+        mm1(5)
+        mm1(4)
+        evac(2)
+        quantize_g(3)
+        turn(3)
+        times_slope(1)
+        silu(2)
         mm1(7)
-        evac(6)
-        turn(5)
-        slope(2)
-        quantize_da(2, 4)
-        times_slope(4)
-        times_slope(5)
-        turn(6)
-        quantize_da(4, 6)
-        evac(7)
-        turn(7)
+        times_slope(0)
+        turn(2)
         slope(3)
+        evac(5)
+        evac(7)
+        turn(5)
+        quantize_da(0, 2)
+        evac(4)
+        mm1(6)
+        times_slope(3)
         mm2(0)
+        evac(6)
+        slope(2)
+        mm2(1)
+        turn(4)
         store_slots(0)
+        times_slope(2)
+        times_slope(5)
+        turn(7)
+        quantize_da(2, 4)
+        turn(6)
+        times_slope(4)
         mm2(3)
-        times_slope(6)
         times_slope(7)
-        quantize_da(6, 7)
+        mm2(2)
+        store_slots_part(1, 1)
+        quantize_da(4, 6)
+        store_slots_part(1, 0)
+        times_slope(6)
+        mm2(5)
         mm2(4)
         quantize_da(7, 8)
-        mm2(2)
-        mm2(5)
-        mm2(6)
-        store_slots_part(3, 0)
+        quantize_da(6, 7)
         mm2(7)
         store_slots(2)
+        mm2(6)
         store_slots_split(3, 1)
-        store_slots(1)
+        store_slots_part(3, 0)
 
         HALF = T // 2
         x1, x2, y = [], [], []

from contextlib import ExitStack

import concourse.mybir as mybir
from concourse.masks import make_identity

K, T, E, C, H, N = 256, 512, 8, 128, 512, 512
S = E * C
FLOPS = 2 * S * (N * H + H * K)
BYTES = 4 * (N * T + H * S + S + K * T) + E * (2 * 128 * H + 16 * H + 2 * 128 * K + 16 * K) + 2 * 128 * (S // 16 + 2 * (T // 16))

F32 = mybir.dt.float32
BF16 = mybir.dt.bfloat16
I32 = mybir.dt.int32
U32 = mybir.dt.uint32
U16 = mybir.dt.uint16
U8 = mybir.dt.uint8
FP8X4 = mybir.dt.float8_e4m3fn_x4
FP4X4 = mybir.dt.float4_e2m1fn_x4

ADD, MULT, SUB = mybir.AluOpType.add, mybir.AluOpType.mult, mybir.AluOpType.subtract
SIGMOID, SILU = mybir.ActivationFunctionType.Sigmoid, mybir.ActivationFunctionType.Silu

P = 128
PACK = 4
CHUNK = 256
RUN = 512
PAD = 32
CHUNKS = S // CHUNK
PER_CHUNK = CHUNK // C


def tile_moe_bdx_mlp_silu_kernel(tc, dyT, a, w2_words, w2_scales, w1_words, w1_scales, gate, offs, pos1, pos2, out):
    nc = tc.nc
    with ExitStack() as ctx:
        lists = ctx.enter_context(tc.tile_pool(name="lists", bufs=1))
        keep = ctx.enter_context(tc.tile_pool(name="keep", bufs=1))
        work = ctx.enter_context(tc.tile_pool(name="work", bufs=3))
        psum = ctx.enter_context(tc.psum_pool(name="psum", bufs=1))

        offs_sb = lists.tile([P, S // 16], U16, name="offs_sb")
        pos1_sb = lists.tile([P, T // 16], U16, name="pos1_sb")
        pos2_sb = lists.tile([P, T // 16], U16, name="pos2_sb")

        warm = keep.tile([P, 8], F32, name="warm")
        nc.vector.memset(warm[:], 0.0)
        warmed = keep.tile([P, 8], F32, name="warmed")
        nc.scalar.activation(warmed[:], warm[:], SIGMOID)

        w2_sb = keep.tile([P, E, 2 * H], U8, name="w2_sb", align_bytes=64)
        w2s_sb = keep.tile([P, E, H], U8, name="w2s_sb", align_bytes=64)
        w1_sb = keep.tile([P, E, 2 * K], U8, name="w1_sb", align_bytes=64)
        w1s_sb = keep.tile([P, E, K], U8, name="w1s_sb", align_bytes=64)
        nc.vector.memset(w2s_sb[:].rearrange("p e i -> p (e i)").bitcast(I32), 0)
        nc.vector.memset(w1s_sb[:].rearrange("p e k -> p (e k)").bitcast(I32), 0)
        ident = keep.tile([P, P], F32, name="ident")
        make_identity(nc, ident[:])

        gate_sb = keep.tile([P, S], F32, name="gate_sb")
        dy = []
        for t in range(PACK):
            dy_t = keep.tile([P, T + PAD], F32, name=f"dy{t}")
            dy.append(dy_t)
        a_sb = keep.tile([P, PACK, S], F32, name="a_sb")
        r_sb = keep.tile([P, PACK, S], F32, name="r_sb")
        s_sb, d_sb = [], []
        for c in range(CHUNKS):
            s_c = keep.tile([P, PACK, CHUNK], F32, name=f"s{c}")
            d_c = keep.tile([P, PACK, CHUNK], F32, name=f"d{c}")
            s_sb.append(s_c)
            d_sb.append(d_c)

        dy_hbm = dyT.rearrange("(p t) s -> p (t s)", t=PACK)
        a_hbm = a.rearrange("(p t) s -> p t s", t=PACK)

        def load_gate(lo, hi):
            nc.sync.dma_start(out=gate_sb[:, lo:hi], in_=gate[0:P, lo:hi])

        def load_dy(t):
            if t < PACK - 1:
                nc.sync.dma_start(out=dy[t][:], in_=dy_hbm[:, t * T : (t + 1) * T + PAD])
            else:
                nc.sync.dma_start(out=dy[t][:, 0:T], in_=dy_hbm[:, t * T : (t + 1) * T])
                nc.sync.dma_start(out=dy[t][:, T : T + PAD], in_=dy_hbm[:, 0:PAD])

        def load_a(t, lo, hi):
            nc.sync.dma_start(out=a_sb[:, t, lo:hi], in_=a_hbm[:, t, lo:hi])

        def load_words(tile, words, lo, hi):
            nc.sync.dma_start(out=tile[:, lo:hi, :].bitcast(I32), in_=words.rearrange("e s p c -> p (e s) c")[:, lo:hi, :].bitcast(I32))

        def load_scales(tile, scales):
            rows = scales.rearrange("e s f i -> f (e s) i")
            for q in range(4):
                nc.sync.dma_start(out=tile[q:P:32, :, :].bitcast(I32), in_=rows[q:16:4, :, :].bitcast(I32))

        load_gate(0 * CHUNK, 1 * CHUNK)
        load_dy(0)
        nc.sync.dma_start(offs_sb[:], offs)
        load_gate(2 * CHUNK, 4 * CHUNK)
        load_gate(1 * CHUNK, 2 * CHUNK)
        load_dy(3)
        load_a(0, 1 * RUN, 2 * RUN)
        load_dy(2)
        load_a(0, 0 * RUN, 1 * RUN)
        load_a(3, 0, S)
        load_a(1, 0, S)
        load_dy(1)
        load_a(2, 0, S)
        load_scales(w2s_sb, w2_scales)
        load_words(w2_sb, w2_words, 0, 2)
        load_words(w2_sb, w2_words, 2, 4)
        load_words(w2_sb, w2_words, 4, 8)
        load_words(w1_sb, w1_words, 0, 8)
        nc.sync.dma_start(pos1_sb[:], pos1)
        nc.sync.dma_start(pos2_sb[:], pos2)
        load_scales(w1s_sb, w1_scales)

        dhT_ps, dhT_sb, dh_ps, dab, daq, das, dx_ps = {}, {}, {}, {}, {}, {}, {}
        g4, gb, gq, gs = {}, {}, {}, {}
        dx_sb = keep.tile([P, 2, S], F32, name="dx_sb")

        def cols(c):
            return slice(c * CHUNK, (c + 1) * CHUNK)

        def g4_of(c):
            return g4[c // 2][:, :, (c % 2) * CHUNK : (c % 2 + 1) * CHUNK]

        def gather(h, t, lo=0, hi=RUN):
            if h not in g4:
                tile = work.tile([P, PACK, RUN], F32, name="g4", bufs=2)
                g4[h] = tile
            nc.vector.tensor_tensor(
                out=g4[h][:, t, lo:hi],
                in0=dy[t][:].indirect(offs_sb[:, (h * RUN + lo) // 16 : (h * RUN + hi) // 16]),
                in1=gate_sb[:, h * RUN + lo : h * RUN + hi],
                op=MULT,
            )

        def new_gb(c):
            tile = work.tile([P, CHUNK, PACK], BF16, name="gb", align_bytes=64)
            gb[c] = tile

        def interleave(c):
            new_gb(c)
            nc.scalar.copy(gb[c][:].rearrange("p (c i) t -> p c t i", i=4), g4_of(c).rearrange("p t (c i) -> p c t i", i=4))

        def interleave_on_vector(c):
            new_gb(c)
            nc.vector.tensor_copy(gb[c][:].rearrange("p (c i) t -> p c t i", i=4), g4_of(c).rearrange("p t (c i) -> p c t i", i=4))

        def quantize_g(c):
            words = work.tile([P, CHUNK], U32, name="gq", align_bytes=64)
            scales = work.tile([P, CHUNK], U8, name="gs", align_bytes=64)
            nc.vector.quantize_mx(out=words[:].bitcast(FP8X4), scales=scales[:], in_=gb[c][:].rearrange("p s t -> p (s t)"))
            gq[c], gs[c] = words, scales

        def sigmoid(t, lo, hi):
            nc.scalar.activation(r_sb[:, t, lo:hi], a_sb[:, t, lo:hi], SIGMOID)

        zero = keep.tile([P, 1], F32, name="zero")

        def tie(t):
            nc.scalar.mul(zero[:], r_sb[:, t, S - 1 : S], 0.0)

        def silu(c):
            nc.scalar.activation(s_sb[c][:], a_sb[:, :, cols(c)], SILU, scale=-1.0, bias=zero[:])

        def slope(c):
            nc.vector.scalar_tensor_tensor(out=d_sb[c][:], in0=s_sb[c][:], scalar=1.0, in1=r_sb[:, :, cols(c)], op0=SUB, op1=MULT)

        def mm1(e):
            c, j = divmod(e, PER_CHUNK)
            tile = psum.tile([P, H], F32, name="dhT_ps", bufs=3)
            nc.tensor.matmul_mx(
                out=tile[:],
                lhsT=gq[c][:, j * C : (j + 1) * C].bitcast(FP8X4),
                lhsT_scale=gs[c][:, j * C : (j + 1) * C],
                rhs=w2_sb[:, e, :].bitcast(FP4X4),
                rhs_scale=w2s_sb[:, e, :],
                start=True,
                stop=True,
            )
            dhT_ps[e] = tile

        def evac(e):
            tile = work.tile([P, PACK, P], F32, name="dhT", bufs=4)
            nc.scalar.copy(tile[:], dhT_ps[e][:].rearrange("s (m t) -> s t m", t=PACK))
            dhT_sb[e] = tile

        def turn(e):
            tile = psum.tile([P, PACK, C], F32, name="dh_ps", bufs=3)
            for t in range(PACK):
                nc.tensor.transpose(tile[:, t, :], dhT_sb[e][:, t, :], ident[:])
            dh_ps[e] = tile

        def times_slope(e):
            c, j = divmod(e, PER_CHUNK)
            if c not in dab:
                tile = work.tile([P, CHUNK, PACK], BF16, name="dab", align_bytes=64)
                dab[c] = tile
            nc.vector.tensor_tensor(
                out=dab[c][:, j * C : (j + 1) * C, :].rearrange("p (c i) t -> p c t i", i=4),
                in0=dh_ps[e][:].rearrange("p t (c i) -> p c t i", i=4),
                in1=d_sb[c][:, :, j * C : (j + 1) * C].rearrange("p t (c i) -> p c t i", i=4),
                op=MULT,
            )

        def quantize_da(lo, hi):
            c = lo // PER_CHUNK
            j = lo % PER_CHUNK
            n = (hi - lo) * C
            words = work.tile([P, CHUNK], U32, name="daq", align_bytes=64)
            scales = work.tile([P, CHUNK], U8, name="das", align_bytes=64)
            nc.vector.quantize_mx(out=words[:, 0:n].bitcast(FP8X4), scales=scales[:, 0:n], in_=dab[c][:, j * C : j * C + n, :].rearrange("p s t -> p (s t)"))
            for e in range(lo, hi):
                daq[e] = words[:, (e - lo) * C : (e - lo + 1) * C]
                das[e] = scales[:, (e - lo) * C : (e - lo + 1) * C]

        def mm2(e):
            c, j = divmod(e, PER_CHUNK)
            if c not in dx_ps:
                tile = psum.tile([P, 2, CHUNK], F32, name="dx_ps", bufs=2)
                dx_ps[c] = tile
            for kt in range(2):
                nc.tensor.matmul_mx(
                    out=dx_ps[c][:, kt, j * C : (j + 1) * C],
                    lhsT=w1_sb[:, e, kt * 2 * P : (kt + 1) * 2 * P].bitcast(FP4X4),
                    lhsT_scale=w1s_sb[:, e, kt * P : (kt + 1) * P],
                    rhs=daq[e].bitcast(FP8X4),
                    rhs_scale=das[e],
                    start=True,
                    stop=True,
                )

        def store_slots(c):
            nc.scalar.mul(dx_sb[:, :, cols(c)], dx_ps[c][:], -1.0)

        def store_slots_part(c, j):
            lo = c * CHUNK + j * C
            nc.scalar.mul(dx_sb[:, :, lo : lo + C], dx_ps[c][:, :, j * C : (j + 1) * C], -1.0)

        def store_slots_split(c, j):
            lo = c * CHUNK + j * C
            nc.vector.tensor_scalar_mul(dx_sb[:, 0, lo : lo + C], dx_ps[c][:, 0, j * C : (j + 1) * C], -1.0)
            nc.scalar.mul(dx_sb[:, 1, lo : lo + C], dx_ps[c][:, 1, j * C : (j + 1) * C], -1.0)

        gather(0, 0, 0 * CHUNK, 1 * CHUNK)
        gather(1, 0)
        gather(1, 3)
        sigmoid(0, 1 * RUN, 2 * RUN)
        gather(1, 2)
        sigmoid(0, 0 * RUN, 1 * RUN)
        gather(0, 2)
        sigmoid(3, 0, S)
        gather(0, 3)
        sigmoid(1, 0, S)
        gather(0, 1)
        tie(3)
        sigmoid(2, 0, S)
        gather(0, 0, 1 * CHUNK, 2 * CHUNK)
        silu(0)
        interleave_on_vector(0)
        interleave_on_vector(1)
        quantize_g(0)
        gather(1, 1)
        mm1(1)
        mm1(0)
        silu(1)
        quantize_g(1)
        interleave_on_vector(2)
        mm1(3)
        interleave_on_vector(3)
        evac(1)
        quantize_g(2)
        evac(0)
        mm1(2)
        slope(0)
        turn(1)
        evac(3)
        turn(0)
        silu(3)
        slope(1)
        mm1(5)
        mm1(4)
        evac(2)
        quantize_g(3)
        turn(3)
        times_slope(1)
        silu(2)
        mm1(7)
        times_slope(0)
        turn(2)
        slope(3)
        evac(5)
        evac(7)
        turn(5)
        quantize_da(0, 2)
        evac(4)
        mm1(6)
        times_slope(3)
        mm2(0)
        evac(6)
        slope(2)
        mm2(1)
        turn(4)
        store_slots(0)
        times_slope(2)
        times_slope(5)
        turn(7)
        quantize_da(2, 4)
        turn(6)
        times_slope(4)
        mm2(3)
        times_slope(7)
        mm2(2)
        store_slots_part(1, 1)
        quantize_da(4, 6)
        store_slots_part(1, 0)
        times_slope(6)
        mm2(5)
        mm2(4)
        quantize_da(7, 8)
        quantize_da(6, 7)
        mm2(7)
        store_slots(2)
        mm2(6)
        store_slots_split(3, 1)
        store_slots_part(3, 0)

        HALF = T // 2
        x1, x2, y = [], [], []
        for kt in range(2):
            x1_k = keep.tile([P, T], F32, name=f"x1_{kt}")
            x2_k = keep.tile([P, T], F32, name=f"x2_{kt}")
            y_k = keep.tile([P, T], F32, name=f"y_{kt}")
            x1.append(x1_k)
            x2.append(x2_k)
            y.append(y_k)
        nc.vector.tensor_copy(x1[0][:], dx_sb[:, 0, :].indirect(pos1_sb[:]))
        nc.vector.tensor_copy(x2[0][:], dx_sb[:, 0, :].indirect(pos2_sb[:]))
        nc.gpsimd.tensor_tensor(out=y[0][:], in0=x1[0][:], in1=x2[0][:], op=ADD)
        nc.sync.dma_start(out=out[0:P, :], in_=y[0][:])
        nc.vector.tensor_copy(x1[1][:], dx_sb[:, 1, :].indirect(pos1_sb[:]))
        for h in range(2):
            tok = slice(h * HALF, (h + 1) * HALF)
            nc.vector.tensor_copy(x2[1][:, tok], dx_sb[:, 1, :].indirect(pos2_sb[:, h * HALF // 16 : (h + 1) * HALF // 16]))
            adder = nc.gpsimd if h == 0 else nc.vector
            adder.tensor_tensor(out=y[1][:, tok], in0=x1[1][:, tok], in1=x2[1][:, tok], op=ADD)
            nc.sync.dma_start(out=out[P : 2 * P, tok], in_=y[1][:, tok])
